import numpy as np
import ml_dtypes


def mxq(x, axis, fmt="e4m3"):
    dtype, down = {"e4m3": (ml_dtypes.float8_e4m3fn, 7), "e5m2": (ml_dtypes.float8_e5m2, 14)}[fmt]
    v = np.moveaxis(np.asarray(x, np.float32).astype(ml_dtypes.bfloat16).astype(np.float64), axis, -1)
    blocks = v.reshape(v.shape[:-1] + (-1, 32))
    amax = np.abs(blocks).max(-1, keepdims=True)
    byte = np.maximum(np.where(amax > 0, np.frexp(amax)[1] - 1 + 127, 0) - down, 1)
    scale = np.exp2(byte - 127.0)
    codes = (blocks / scale).astype(np.float32).astype(dtype).astype(np.float64)
    return np.moveaxis((codes * scale).reshape(v.shape), -1, axis)


WIDE = False


def mx_kscale(k):
    if not WIDE:
        return np.ones(k)
    levels = np.array([10, -10, 5, -5, 0])
    if k % 512:
        return np.exp2(np.random.permutation(np.resize(levels, k // 32))).repeat(32)
    a = np.empty((k // 512, 16))
    for p in range(k // 512):
        a[p, :8] = np.random.permutation(np.resize(levels, 8))
        for g in range(8):
            far = levels[np.abs(levels - a[p, g]) >= 10]
            a[p, g + 8] = far[np.random.randint(len(far))]
    return np.exp2(a.ravel()).repeat(32)


def f64(x):
    return np.asarray(x).astype(np.float64)


def striped(idx):
    return np.tile(np.asarray(idx).reshape(-1, 16).T, (8, 1)).astype(np.uint16)


def unstriped(offs):
    return offs[:16].T.reshape(-1).astype(np.int64)


def striped8(idx):
    return np.asarray(idx).reshape(8, -1, 16).transpose(0, 2, 1).reshape(128, -1).astype(np.uint16)


def unstriped8(offs):
    return offs.reshape(8, 16, -1).transpose(0, 2, 1).reshape(8, -1).astype(np.int64)


def pick8(x, idx, run):
    r = np.arange(len(x))
    return x[r[:, None], idx[r % (8 * run) // run]]


E2M1 = np.array([0.0, 0.5, 1.0, 1.5, 2.0, 3.0, 4.0, 6.0, -0.0, -0.5, -1.0, -1.5, -2.0, -3.0, -4.0, -6.0])


def pack_weight(w, fmt):
    k, n = w.shape
    w = f64(np.asarray(w, np.float32).astype(ml_dtypes.bfloat16)).reshape(k // 32, 32, n)
    amax = np.abs(w).max(1)
    if fmt == "e4m3":
        byte = np.frexp(amax)[1] - 1 + 127 - 7
    else:
        mant, ex = np.frexp(amax / 6.0)
        byte = np.where(mant > 0.5, ex, ex - 1) + 127
    byte = np.clip(np.where(amax > 0, byte, 1), 1, 254)
    scaled = (w * np.exp2(127.0 - byte)[:, None, :]).reshape(k, n).astype(np.float32)
    by_word = np.ascontiguousarray(scaled.reshape(k // 512, 128, 4, n).transpose(0, 1, 3, 2))
    if fmt == "e4m3":
        words = by_word.astype(ml_dtypes.float8_e4m3fn).view(np.uint8)
    else:
        c = by_word.astype(ml_dtypes.float4_e2m1fn).view(np.uint8) & 0xF
        words = (c[..., 0::2] | (c[..., 1::2] << 4)).reshape(k // 512, 128, 2 * n)
    return np.ascontiguousarray(words), np.ascontiguousarray(byte.astype(np.uint8).reshape(k // 512, 16, n))


def unpack_weight(words, scales, fmt):
    g, _, n = scales.shape
    words = np.ascontiguousarray(words).reshape(g, 128, n, -1)
    if fmt == "e4m3":
        vals = words.view(ml_dtypes.float8_e4m3fn).astype(np.float64)
    else:
        nib = np.empty((g, 128, n, 4), np.uint8)
        nib[..., 0::2] = words & 0xF
        nib[..., 1::2] = words >> 4
        vals = E2M1[nib]
    vals = vals * np.repeat(np.exp2(scales.astype(np.float64) - 127.0), 8, axis=1)[..., None]
    return vals.transpose(0, 1, 3, 2).reshape(g * 512, n)


K, J, R, T, Z, M, C, O, S, N = 512, 512, 512, 2048, 512, 1024, 1024, 512, 256, 256


def setup_inputs():
    n = np.random.standard_normal
    idx = np.random.permutation(T)[:J]
    idx2 = np.random.permutation(M)[:J]
    idx3 = np.stack([np.random.permutation(C)[:J] for _ in range(8)])
    idx4 = np.stack([np.random.permutation(J)[:S] for _ in range(8)])
    idx5 = np.stack([np.random.permutation(C)[:S] for _ in range(8)])
    idx6 = np.stack([np.random.permutation(C)[:O] for _ in range(8)])
    fk = mx_kscale(K)
    fr = mx_kscale(R)
    fz = mx_kscale(Z)
    xtp = pack_weight(n((K, T)) * fk[:, None], "e4m3")
    wp = pack_weight(n((K, R)) * 1 / np.sqrt(K) / fk[:, None] * fr, "e2m1")
    xop = pack_weight(n((Z, M)) / fz[:, None], "e2m1")
    w2p = pack_weight(n((Z, R)) * 1 / np.sqrt(Z) * fz[:, None] * fr, "e4m3")
    wbp = pack_weight(n((R, N)) * 1 / np.sqrt(R) / fr[:, None], "e4m3")
    return {
        "xt_words": xtp[0],
        "xt_scales": xtp[1],
        "w_words": wp[0],
        "w_scales": wp[1],
        "xo_words": xop[0],
        "xo_scales": xop[1],
        "w2_words": w2p[0],
        "w2_scales": w2p[1],
        "sa": (np.random.uniform(0.5, 1.6, (R, 1))).astype(np.float32),
        "sb": (np.random.uniform(0.5, 1.6, (R, 1))).astype(np.float32),
        "wb_words": wbp[0],
        "wb_scales": wbp[1],
        "offs": striped(idx),
        "offs2": striped(idx2),
        "offs3": striped8(idx3),
        "offs4": striped8(idx4),
        "offs5": striped8(idx5),
        "offs6": striped8(idx6),
    }


def reference(xt_words, xt_scales, w_words, w_scales, xo_words, xo_scales, w2_words, w2_scales, sa, sb, wb_words, wb_scales, offs, offs2, offs3, offs4, offs5, offs6):
    idx = unstriped(offs)
    idx2 = unstriped(offs2)
    idx3 = unstriped8(offs3)
    idx4 = unstriped8(offs4)
    idx5 = unstriped8(offs5)
    idx6 = unstriped8(offs6)
    xtu = unpack_weight(xt_words, xt_scales, "e4m3")
    wu = unpack_weight(w_words, w_scales, "e2m1")
    xou = unpack_weight(xo_words, xo_scales, "e2m1")
    w2u = unpack_weight(w2_words, w2_scales, "e4m3")
    wbu = unpack_weight(wb_words, wb_scales, "e4m3")
    xtidxg = xtu[:, idx]
    xoidx2g = xou[:, idx2]
    a = wu.T @ xtidxg + w2u.T @ xoidx2g
    pw = np.zeros((R, C))
    pw[np.arange(R)[:, None], idx3[np.arange(R) % 512 // 64]] = a
    h1 = pick8(a, idx4, 64) * f64(sa)
    pv = np.zeros((R, C))
    pv[np.arange(R)[:, None], idx5[np.arange(R) % 512 // 64]] = h1
    pb = np.max(pv, axis=1, keepdims=True)
    pg = np.maximum(pw, pv - pb)
    hid = pick8(pg, idx6, 64) * f64(sb)
    hidq = mxq(hid, 0, "e4m3")
    y = wbu.T @ hidq
    return y

@@ -1,0 +1,248 @@
+from contextlib import ExitStack
+
+import concourse.mybir as mybir
+
+F32 = mybir.dt.float32
+BF16 = mybir.dt.bfloat16
+I32 = mybir.dt.int32
+U32 = mybir.dt.uint32
+U16 = mybir.dt.uint16
+U8 = mybir.dt.uint8
+FP8X4 = mybir.dt.float8_e4m3fn_x4
+FP4X4 = mybir.dt.float4_e2m1fn_x4
+COPY = mybir.ActivationFunctionType.Copy
+ALU = mybir.AluOpType
+AXIS_X = mybir.AxisListType.X
+
+P = 128
+PACK = 4
+QUADS = 4
+K, J, R, T, M, C, O, S, N = 512, 512, 512, 2048, 1024, 1024, 512, 256, 256
+HALF = 256
+GROUP = 16
+
+FLOPS = 2 * K * R * J * 2 + 2 * R * N * O
+
+
+def tile_picked_tokens_plain_bank_belowbest_one_plain_kernel(
+    tc, xt_words, xt_scales, w_words, w_scales, xo_words, xo_scales, w2_words, w2_scales,
+    sa, sb, wb_words, wb_scales, offs, offs2, offs3, offs4, offs5, offs6, out,
+):
+    nc = tc.nc
+    with ExitStack() as ctx:
+        keep = ctx.enter_context(tc.tile_pool(name="keep", bufs=1))
+        psum = ctx.enter_context(tc.psum_pool(name="psum", bufs=1))
+
+        def sb_tile(name, shape, dtype, tag=None):
+            return keep.tile(shape, dtype, name=name, tag=tag or name, align_bytes=64)
+
+        def load_list(name, src):
+            lst = keep.tile([P, src.shape[1]], U16, name=name)
+            nc.sync.dma_start(lst[:], src)
+            return lst
+
+        def entries(lst, first, count):
+            return lst[:, first // GROUP : (first + count) // GROUP]
+
+        def rows_by_quadrant(scales):
+            return scales[0].rearrange("(q i) c -> i q c", i=PACK).bitcast(I32)
+
+        def load_plane(plane, scales):
+            for q in range(QUADS):
+                nc.sync.dma_start(
+                    plane[32 * q : 32 * q + PACK, :].bitcast(I32),
+                    scales[0, PACK * q : PACK * (q + 1), :].bitcast(I32),
+                )
+
+        def spread(plane, stage):
+            for q in range(QUADS):
+                nc.vector.tensor_copy(plane[32 * q : 32 * q + PACK, :].bitcast(I32), stage[:, q, :])
+
+        xt_plane = sb_tile("xt_plane", [P, T], U8)
+        xo_plane = sb_tile("xo_plane", [P, M], U8)
+        ww_plane = sb_tile("ww_plane", [P, 2 * R], U8)
+        wb_plane = sb_tile("wb_plane", [P, N], U8)
+        for plane in (xt_plane, xo_plane, ww_plane):
+            nc.vector.memset(plane[:].bitcast(I32), 0)
+
+        xo_stage = sb_tile("xo_stage", [PACK, QUADS, M // 4], I32)
+        ww_stage = sb_tile("ww_stage", [PACK, QUADS, 2 * R // 4], I32)
+        nc.sync.dma_start(xo_stage[:], rows_by_quadrant(xo_scales))
+        nc.sync.dma_start(ww_stage[:, :, : R // 4], rows_by_quadrant(w2_scales))
+        nc.sync.dma_start(ww_stage[:, :, R // 4 :], rows_by_quadrant(w_scales))
+        notes_list = load_list("notes_list", offs2)
+        tokens_list = load_list("tokens_list", offs)
+
+        xo_table = sb_tile("xo_table", [P, M], U16)
+        w2_raw = sb_tile("w2_raw", [P, R], U32)
+        w_raw = sb_tile("w_raw", [P, R], U16)
+        xt_table = sb_tile("xt_table", [P, T], U32)
+        nc.sync.dma_start(xo_table[:].bitcast(I32), xo_words[0].bitcast(I32))
+        nc.sync.dma_start(w2_raw[:].bitcast(I32), w2_words[0].rearrange("p c b -> p (c b)").bitcast(I32))
+        nc.sync.dma_start(w_raw[:].bitcast(I32), w_words[0].bitcast(I32))
+        load_plane(xt_plane, xt_scales)
+        nc.sync.dma_start(xt_table[:].bitcast(I32), xt_words[0].rearrange("p c b -> p (c b)").bitcast(I32))
+
+        board_list = load_list("board_list", offs3)
+        slot_list = load_list("slot_list", offs4)
+        sa_cols = sb_tile("sa_cols", [P, PACK], F32)
+        nc.sync.dma_start(sa_cols[:], sa.rearrange("(p t) o -> p (t o)", t=PACK))
+        marks_list = load_list("marks_list", offs5)
+        places_list = load_list("places_list", offs6)
+        sb_cols = sb_tile("sb_cols", [P, PACK], F32)
+        nc.sync.dma_start(sb_cols[:], sb.rearrange("(p t) o -> p (t o)", t=PACK))
+
+        spread(xo_plane, xo_stage)
+        spread(ww_plane, ww_stage)
+
+        w2_dealt = sb_tile("w2_dealt", [P, PACK, P], U32)
+        w_dealt = sb_tile("w_dealt", [P, PACK, P], U16)
+        nc.scalar.copy(w2_dealt[:], w2_raw[:].rearrange("p (m t) -> p t m", t=PACK))
+        nc.scalar.copy(w_dealt[:], w_raw[:].rearrange("p (m t) -> p t m", t=PACK))
+        ww_bytes = []
+        for t in range(PACK):
+            dealt = sb_tile("ww_bytes%d" % t, [P, 2, P], U8)
+            nc.gpsimd.tensor_copy(dealt[:], ww_plane[:].rearrange("p (a m t) -> p t a m", a=2, t=PACK)[:, t])
+            ww_bytes.append(dealt)
+
+        pw = [sb_tile("pw%d" % b, [P, C], F32) for b in range(2)]
+        pv = [sb_tile("pv%d" % b, [P, C], F32) for b in range(2)]
+        for board in pw:
+            nc.vector.memset(board[:], 0.0)
+
+        picked = []
+
+        def gather_half(h):
+            xo_b = sb_tile("xo_b%d" % h, [P, HALF], U8)
+            xo_w = sb_tile("xo_w%d" % h, [P, HALF], U16)
+            xt_b = sb_tile("xt_b%d" % h, [P, HALF], U8)
+            xt_w = sb_tile("xt_w%d" % h, [P, HALF], U32)
+            notes = entries(notes_list, h * HALF, HALF)
+            tokens = entries(tokens_list, h * HALF, HALF)
+            nc.vector.tensor_copy(xo_b[:], xo_plane[:].indirect(notes))
+            nc.vector.tensor_copy(xo_w[:], xo_table[:].indirect(notes))
+            nc.vector.tensor_copy(xt_b[:], xt_plane[:].indirect(tokens))
+            nc.vector.tensor_copy(xt_w[:], xt_table[:].indirect(tokens))
+            picked.append((xo_w, xo_b, xt_w, xt_b))
+
+        a = [sb_tile("a%d" % t, [P, J], F32) for t in range(PACK)]
+
+        def hidden(t, h, copy_out):
+            xo_w, xo_b, xt_w, xt_b = picked[h]
+            acc = psum.tile([P, HALF], F32, name="acc", tag="acc", bufs=4)
+            nc.tensor.matmul_mx(
+                acc[:], lhsT=w2_dealt[:, t, :].bitcast(FP8X4), lhsT_scale=ww_bytes[t][:, 0, :],
+                rhs=xo_w[:].bitcast(FP4X4), rhs_scale=xo_b[:], start=True, stop=False,
+            )
+            nc.tensor.matmul_mx(
+                acc[:], lhsT=w_dealt[:, t, :].bitcast(FP4X4), lhsT_scale=ww_bytes[t][:, 1, :],
+                rhs=xt_w[:].bitcast(FP8X4), rhs_scale=xt_b[:], start=False, stop=True,
+            )
+            copy_out(a[t][:, h * HALF : (h + 1) * HALF], acc[:])
+
+        def put_board(t, first, count):
+            nc.scalar.activation(
+                pw[t % 2][:].indirect(entries(board_list, first, count)), a[t][:, first : first + count], COPY
+            )
+
+        h1 = {}
+
+        def take_marks(t):
+            h1[t] = sb_tile("h1_%d" % t, [P, S], F32)
+            nc.scalar.activation(h1[t][:], a[t][:].indirect(slot_list[:]), COPY, scale=sa_cols[:, t : t + 1])
+
+        def put_marks(t):
+            nc.scalar.activation(pv[t % 2][:].indirect(marks_list[:]), h1[t][:], COPY)
+
+        pb = {}
+        pg = {}
+
+        def row_top(t):
+            pb[t] = sb_tile("pb%d" % t, [P, 1], F32)
+            nc.vector.tensor_reduce(pb[t][:], pv[t % 2][:], AXIS_X, ALU.max)
+
+        def merge(t):
+            pg[t] = sb_tile("pg%d" % t, [P, C], F32)
+            nc.vector.scalar_tensor_tensor(
+                pg[t][:], pv[t % 2][:], pb[t][:], pw[t % 2][:], ALU.subtract, ALU.max
+            )
+
+        hid = {}
+
+        def read_places(t, h):
+            nc.scalar.activation(
+                hid[h][:, t, :], pg[t][:].indirect(entries(places_list, h * HALF, HALF)), COPY,
+                scale=sb_cols[:, t : t + 1],
+            )
+
+        gather_half(0)
+        hidden(0, 0, nc.scalar.copy)
+        hidden(1, 0, nc.vector.tensor_copy)
+        put_board(0, 0, HALF)
+        put_board(1, 0, HALF)
+        gather_half(1)
+        hidden(0, 1, nc.vector.tensor_copy)
+        hidden(1, 1, nc.vector.tensor_copy)
+        for board in pv:
+            nc.vector.memset(board[:], 0.0)
+        for t in (2, 3):
+            for h in range(2):
+                hidden(t, h, nc.vector.tensor_copy)
+
+        wb_codes = sb_tile("wb_codes", [P, N], U32)
+        nc.sync.dma_start(wb_codes[:].bitcast(I32), wb_words[0].rearrange("p c b -> p (c b)").bitcast(I32))
+        nc.vector.memset(wb_plane[:].bitcast(I32), 0)
+        load_plane(wb_plane, wb_scales)
+
+        hid[0] = sb_tile("hid0", [P, PACK, HALF], BF16)
+        for t in (0, 1):
+            take_marks(t)
+            put_board(t, HALF, HALF)
+            put_marks(t)
+            row_top(t)
+            merge(t)
+        read_places(0, 0)
+        take_marks(2)
+        put_board(2, 0, J)
+        put_marks(2)
+        row_top(2)
+        merge(2)
+        take_marks(3)
+        read_places(1, 0)
+        put_marks(3)
+        row_top(3)
+        read_places(2, 0)
+        put_board(3, 0, J)
+        merge(3)
+
+        hid[1] = sb_tile("hid1", [P, PACK, HALF], BF16, tag="h1_3")
+        for t in range(PACK - 1):
+            read_places(t, 1)
+
+        def finish(h):
+            woven = sb_tile("woven%d" % h, [P, HALF, PACK], BF16)
+            nc.vector.tensor_copy(
+                woven[:].rearrange("p (c i) t -> p c t i", i=PACK),
+                hid[h][:].rearrange("p t (c i) -> p c t i", i=PACK),
+            )
+            codes = sb_tile("codes%d" % h, [P, HALF], U32)
+            plane = sb_tile("plane%d" % h, [P, HALF], U8)
+            nc.vector.quantize_mx(codes[:].bitcast(FP8X4), plane[:], woven[:].rearrange("p c t -> p (c t)"))
+            for b in range(N // P):
+                rows = slice(b * P, (b + 1) * P)
+                res = psum.tile([P, HALF], F32, name="res", tag="res", bufs=4)
+                nc.tensor.matmul_mx(
+                    res[:], lhsT=wb_codes[:, rows].bitcast(FP8X4), lhsT_scale=wb_plane[:, rows],
+                    rhs=codes[:].bitcast(FP8X4), rhs_scale=plane[:], start=True, stop=True,
+                )
+                staged = sb_tile("staged%d_%d" % (h, b), [P, HALF], F32)
+                if h == 1 and b == 0:
+                    nc.scalar.copy(staged[:], res[:])
+                else:
+                    nc.vector.tensor_copy(staged[:], res[:])
+                nc.sync.dma_start(out[rows, h * HALF : (h + 1) * HALF], staged[:])
+
+        for h in range(2):
+            read_places(PACK - 1, h)
+        for h in range(2):
+            finish(h)

@@ -20,6 +20,8 @@ QUADS = 4
 K, J, R, T, M, C, O, S, N = 512, 512, 512, 2048, 1024, 1024, 512, 256, 256
 HALF = 256
 GROUP = 16
+BOARD_BYTES = 4 * C
+MARKS_AT = 3 * BOARD_BYTES
 
 FLOPS = 2 * K * R * J * 2 + 2 * R * N * O
 
@@ -31,10 +33,14 @@ def tile_picked_tokens_plain_bank_belowbest_one_plain_kernel(
     nc = tc.nc
     with ExitStack() as ctx:
         keep = ctx.enter_context(tc.tile_pool(name="keep", bufs=1))
+        shared = ctx.enter_context(tc.tile_pool(name="shared", bufs=1))
         psum = ctx.enter_context(tc.psum_pool(name="psum", bufs=1))
 
         def sb_tile(name, shape, dtype, tag=None):
             return keep.tile(shape, dtype, name=name, tag=tag or name, align_bytes=64)
+
+        def placed(name, shape, dtype, offset):
+            return shared.tile(shape, dtype, name=name, align_bytes=64, offset=offset)
 
         def load_list(name, src):
             lst = keep.tile([P, src.shape[1]], U16, name=name)
@@ -56,20 +62,23 @@ def tile_picked_tokens_plain_bank_belowbest_one_plain_kernel(
 
         def spread(plane, stage):
             for q in range(QUADS):
-                nc.vector.tensor_copy(plane[32 * q : 32 * q + PACK, :].bitcast(I32), stage[:, q, :])
+                rows = plane[32 * q : 32 * q + PACK, :].bitcast(I32)
+                nc.vector.tensor_copy(rows.rearrange("p (a c) -> p a c", a=stage.shape[1]), stage[:, :, q, :])
 
         xt_plane = sb_tile("xt_plane", [P, T], U8)
         xo_plane = sb_tile("xo_plane", [P, M], U8)
         ww_plane = sb_tile("ww_plane", [P, 2 * R], U8)
         wb_plane = sb_tile("wb_plane", [P, N], U8)
-        for plane in (xt_plane, xo_plane, ww_plane):
+        nc.vector.memset(xt_plane[:, : T // 2].bitcast(I32), 0)
+        nc.gpsimd.memset(xt_plane[:, T // 2 :].bitcast(I32), 0)
+        for plane in (xo_plane, ww_plane):
             nc.vector.memset(plane[:].bitcast(I32), 0)
 
-        xo_stage = sb_tile("xo_stage", [PACK, QUADS, M // 4], I32)
-        ww_stage = sb_tile("ww_stage", [PACK, QUADS, 2 * R // 4], I32)
-        nc.sync.dma_start(xo_stage[:], rows_by_quadrant(xo_scales))
-        nc.sync.dma_start(ww_stage[:, :, : R // 4], rows_by_quadrant(w2_scales))
-        nc.sync.dma_start(ww_stage[:, :, R // 4 :], rows_by_quadrant(w_scales))
+        xo_stage = sb_tile("xo_stage", [PACK, 1, QUADS, M // 4], I32)
+        ww_stage = sb_tile("ww_stage", [PACK, 2, QUADS, R // 4], I32)
+        nc.sync.dma_start(xo_stage[:, 0], rows_by_quadrant(xo_scales))
+        nc.sync.dma_start(ww_stage[:, 0], rows_by_quadrant(w2_scales))
+        nc.sync.dma_start(ww_stage[:, 1], rows_by_quadrant(w_scales))
         notes_list = load_list("notes_list", offs2)
         tokens_list = load_list("tokens_list", offs)
 
@@ -92,8 +101,8 @@ def tile_picked_tokens_plain_bank_belowbest_one_plain_kernel(
         sb_cols = sb_tile("sb_cols", [P, PACK], F32)
         nc.sync.dma_start(sb_cols[:], sb.rearrange("(p t) o -> p (t o)", t=PACK))
 
-        spread(xo_plane, xo_stage)
         spread(ww_plane, ww_stage)
+        spread(xo_plane, xo_stage)
 
         w2_dealt = sb_tile("w2_dealt", [P, PACK, P], U32)
         w_dealt = sb_tile("w_dealt", [P, PACK, P], U16)
@@ -106,17 +115,23 @@ def tile_picked_tokens_plain_bank_belowbest_one_plain_kernel(
             ww_bytes.append(dealt)
 
         pw = [sb_tile("pw%d" % b, [P, C], F32) for b in range(2)]
-        pv = [sb_tile("pv%d" % b, [P, C], F32) for b in range(2)]
-        for board in pw:
-            nc.vector.memset(board[:], 0.0)
+        nc.vector.memset(pw[0][:], 0.0)
+        nc.gpsimd.memset(pw[1][:], 0.0)
 
+        pv = []
         picked = []
 
         def gather_half(h):
-            xo_b = sb_tile("xo_b%d" % h, [P, HALF], U8)
-            xo_w = sb_tile("xo_w%d" % h, [P, HALF], U16)
-            xt_b = sb_tile("xt_b%d" % h, [P, HALF], U8)
-            xt_w = sb_tile("xt_w%d" % h, [P, HALF], U32)
+            if h == 0:
+                xo_b = placed("xo_b0", [P, HALF], U8, 0)
+                xo_w = placed("xo_w0", [P, HALF], U16, HALF)
+                xt_b = placed("xt_b0", [P, HALF], U8, BOARD_BYTES)
+                xt_w = placed("xt_w0", [P, HALF], U32, 2 * BOARD_BYTES)
+            else:
+                xo_b = placed("xo_b1", [P, HALF], U8, 2 * BOARD_BYTES)
+                xo_w = placed("xo_w1", [P, HALF], U16, 2 * BOARD_BYTES + HALF)
+                xt_b = placed("xt_b1", [P, HALF], U8, 2 * BOARD_BYTES + 3 * HALF)
+                xt_w = sb_tile("xt_w1", [P, HALF], U32)
             notes = entries(notes_list, h * HALF, HALF)
             tokens = entries(tokens_list, h * HALF, HALF)
             nc.vector.tensor_copy(xo_b[:], xo_plane[:].indirect(notes))
@@ -142,13 +157,16 @@ def tile_picked_tokens_plain_bank_belowbest_one_plain_kernel(
 
         def put_board(t, first, count):
             nc.scalar.activation(
-                pw[t % 2][:].indirect(entries(board_list, first, count)), a[t][:, first : first + count], COPY
+                pw[t][:].indirect(entries(board_list, first, count)), a[t][:, first : first + count], COPY
             )
 
         h1 = {}
 
         def take_marks(t):
-            h1[t] = sb_tile("h1_%d" % t, [P, S], F32)
+            if t == PACK - 1:
+                h1[t] = placed("h1_last", [P, S], F32, MARKS_AT + 2 * HALF)
+            else:
+                h1[t] = sb_tile("h1_%d" % t, [P, S], F32)
             nc.scalar.activation(h1[t][:], a[t][:].indirect(slot_list[:]), COPY, scale=sa_cols[:, t : t + 1])
 
         def put_marks(t):
@@ -158,76 +176,38 @@ def tile_picked_tokens_plain_bank_belowbest_one_plain_kernel(
         pg = {}
 
         def row_top(t):
+            top = sb_tile("top%d" % t, [P, 1], F32)
             pb[t] = sb_tile("pb%d" % t, [P, 1], F32)
-            nc.vector.tensor_reduce(pb[t][:], pv[t % 2][:], AXIS_X, ALU.max)
+            nc.vector.tensor_reduce(top[:], h1[t][:], AXIS_X, ALU.max)
+            nc.vector.tensor_scalar_max(pb[t][:], top[:], 0.0)
 
         def merge(t):
             pg[t] = sb_tile("pg%d" % t, [P, C], F32)
             nc.vector.scalar_tensor_tensor(
-                pg[t][:], pv[t % 2][:], pb[t][:], pw[t % 2][:], ALU.subtract, ALU.max
+                pg[t][:], pv[t % 2][:], pb[t][:], pw[t][:], ALU.subtract, ALU.max
             )
 
         hid = {}
 
         def read_places(t, h):
             nc.scalar.activation(
-                hid[h][:, t, :], pg[t][:].indirect(entries(places_list, h * HALF, HALF)), COPY,
+                hid[h, t // 2][:, t % 2, :], pg[t][:].indirect(entries(places_list, h * HALF, HALF)), COPY,
                 scale=sb_cols[:, t : t + 1],
             )
 
-        gather_half(0)
-        hidden(0, 0, nc.scalar.copy)
-        hidden(1, 0, nc.vector.tensor_copy)
-        put_board(0, 0, HALF)
-        put_board(1, 0, HALF)
-        gather_half(1)
-        hidden(0, 1, nc.vector.tensor_copy)
-        hidden(1, 1, nc.vector.tensor_copy)
-        for board in pv:
-            nc.vector.memset(board[:], 0.0)
-        for t in (2, 3):
-            for h in range(2):
-                hidden(t, h, nc.vector.tensor_copy)
+        woven = {}
 
-        wb_codes = sb_tile("wb_codes", [P, N], U32)
-        nc.sync.dma_start(wb_codes[:].bitcast(I32), wb_words[0].rearrange("p c b -> p (c b)").bitcast(I32))
-        nc.vector.memset(wb_plane[:].bitcast(I32), 0)
-        load_plane(wb_plane, wb_scales)
-
-        hid[0] = sb_tile("hid0", [P, PACK, HALF], BF16)
-        for t in (0, 1):
-            take_marks(t)
-            put_board(t, HALF, HALF)
-            put_marks(t)
-            row_top(t)
-            merge(t)
-        read_places(0, 0)
-        take_marks(2)
-        put_board(2, 0, J)
-        put_marks(2)
-        row_top(2)
-        merge(2)
-        take_marks(3)
-        read_places(1, 0)
-        put_marks(3)
-        row_top(3)
-        read_places(2, 0)
-        put_board(3, 0, J)
-        merge(3)
-
-        hid[1] = sb_tile("hid1", [P, PACK, HALF], BF16, tag="h1_3")
-        for t in range(PACK - 1):
-            read_places(t, 1)
+        def weave(h, pair):
+            if pair == 0:
+                woven[h] = sb_tile("woven%d" % h, [P, HALF, PACK], BF16)
+            nc.vector.tensor_copy(
+                woven[h][:, :, 2 * pair : 2 * pair + 2], hid[h, pair][:].rearrange("p t c -> p c t")
+            )
 
         def finish(h):
-            woven = sb_tile("woven%d" % h, [P, HALF, PACK], BF16)
-            nc.vector.tensor_copy(
-                woven[:].rearrange("p (c i) t -> p c t i", i=PACK),
-                hid[h][:].rearrange("p t (c i) -> p c t i", i=PACK),
-            )
             codes = sb_tile("codes%d" % h, [P, HALF], U32)
             plane = sb_tile("plane%d" % h, [P, HALF], U8)
-            nc.vector.quantize_mx(codes[:].bitcast(FP8X4), plane[:], woven[:].rearrange("p c t -> p (c t)"))
+            nc.vector.quantize_mx(codes[:].bitcast(FP8X4), plane[:], woven[h][:].rearrange("p c t -> p (c t)"))
             for b in range(N // P):
                 rows = slice(b * P, (b + 1) * P)
                 res = psum.tile([P, HALF], F32, name="res", tag="res", bufs=4)
@@ -236,13 +216,57 @@ def tile_picked_tokens_plain_bank_belowbest_one_plain_kernel(
                     rhs=codes[:].bitcast(FP8X4), rhs_scale=plane[:], start=True, stop=True,
                 )
                 staged = sb_tile("staged%d_%d" % (h, b), [P, HALF], F32)
-                if h == 1 and b == 0:
-                    nc.scalar.copy(staged[:], res[:])
-                else:
+                if h == 1 and b == 1:
                     nc.vector.tensor_copy(staged[:], res[:])
+                else:
+                    nc.scalar.copy(staged[:], res[:])
                 nc.sync.dma_start(out[rows, h * HALF : (h + 1) * HALF], staged[:])
 
+        gather_half(0)
+        hidden(0, 0, nc.scalar.copy)
+        for t in range(1, PACK):
+            hidden(t, 0, nc.vector.tensor_copy)
+        for b in range(2):
+            pw.append(placed("pw%d" % (2 + b), [P, C], F32, b * BOARD_BYTES))
+            nc.gpsimd.memset(pw[2 + b][:], 0.0)
+        for t in range(PACK):
+            put_board(t, 0, HALF)
+        gather_half(1)
+        hidden(0, 1, nc.vector.tensor_copy)
+        pv.append(sb_tile("pv0", [P, C], F32, tag="xo_table"))
+        nc.gpsimd.memset(pv[0][:], 0.0)
+        hidden(1, 1, nc.vector.tensor_copy)
+        for t in (2, 3):
+            hidden(t, 1, nc.vector.tensor_copy)
+        pv.append(placed("pv1", [P, C], F32, 2 * BOARD_BYTES))
+        nc.gpsimd.memset(pv[1][:], 0.0)
+
+        wb_codes = sb_tile("wb_codes", [P, N], U32)
+        nc.sync.dma_start(wb_codes[:].bitcast(I32), wb_words[0].rearrange("p c b -> p (c b)").bitcast(I32))
+        nc.vector.memset(wb_plane[:].bitcast(I32), 0)
+        load_plane(wb_plane, wb_scales)
+
+        hid[0, 0] = sb_tile("hid00", [P, 2, HALF], BF16)
+        for t in range(PACK):
+            take_marks(t)
+            row_top(t)
+            put_board(t, HALF, HALF)
+            put_marks(t)
+            merge(t)
+            if t in (1, 2):
+                read_places(t - 1, 0)
+        weave(0, 0)
+
+        hid[1, 0] = placed("hid10", [P, 2, HALF], BF16, MARKS_AT)
+        hid[0, 1] = placed("hid01", [P, 2, HALF], BF16, MARKS_AT + 4 * HALF)
+        hid[1, 1] = sb_tile("hid11", [P, 2, HALF], BF16, tag="pb3")
+        read_places(0, 1)
+        read_places(1, 1)
+        read_places(2, 0)
+        read_places(3, 0)
+        read_places(2, 1)
+        read_places(3, 1)
+        weave(1, 0)
         for h in range(2):
-            read_places(PACK - 1, h)
-        for h in range(2):
+            weave(h, 1)
             finish(h)

@@ -20,6 +20,7 @@ QUADS = 4
 K, J, R, T, M, C, O, S, N = 512, 512, 512, 2048, 1024, 1024, 512, 256, 256
 HALF = 256
 GROUP = 16
+QUARTER = 128
 BOARD_BYTES = 4 * C
 MARKS_AT = 3 * BOARD_BYTES
 
@@ -60,10 +61,9 @@ def tile_picked_tokens_plain_bank_belowbest_one_plain_kernel(
                     scales[0, PACK * q : PACK * (q + 1), :].bitcast(I32),
                 )
 
-        def spread(plane, stage):
-            for q in range(QUADS):
-                rows = plane[32 * q : 32 * q + PACK, :].bitcast(I32)
-                nc.vector.tensor_copy(rows.rearrange("p (a c) -> p a c", a=stage.shape[1]), stage[:, :, q, :])
+        def spread(plane, stage, q):
+            rows = plane[32 * q : 32 * q + PACK, :].bitcast(I32)
+            nc.vector.tensor_copy(rows.rearrange("p (a c) -> p a c", a=stage.shape[1]), stage[:, :, q, :])
 
         xt_plane = sb_tile("xt_plane", [P, T], U8)
         xo_plane = sb_tile("xo_plane", [P, M], U8)
@@ -101,8 +101,9 @@ def tile_picked_tokens_plain_bank_belowbest_one_plain_kernel(
         sb_cols = sb_tile("sb_cols", [P, PACK], F32)
         nc.sync.dma_start(sb_cols[:], sb.rearrange("(p t) o -> p (t o)", t=PACK))
 
-        spread(ww_plane, ww_stage)
-        spread(xo_plane, xo_stage)
+        for q in range(QUADS):
+            spread(xo_plane, xo_stage, q)
+            spread(ww_plane, ww_stage, q)
 
         w2_dealt = sb_tile("w2_dealt", [P, PACK, P], U32)
         w_dealt = sb_tile("w_dealt", [P, PACK, P], U16)
@@ -124,36 +125,45 @@ def tile_picked_tokens_plain_bank_belowbest_one_plain_kernel(
         def gather_half(h):
             if h == 0:
                 xo_b = placed("xo_b0", [P, HALF], U8, 0)
-                xo_w = placed("xo_w0", [P, HALF], U16, HALF)
-                xt_b = placed("xt_b0", [P, HALF], U8, BOARD_BYTES)
+                xo_w = placed("xo_w0", [P, HALF], U16, BOARD_BYTES)
+                xt_b = placed("xt_b0", [P, HALF], U8, 2 * BOARD_BYTES + 4 * HALF)
                 xt_w = placed("xt_w0", [P, HALF], U32, 2 * BOARD_BYTES)
             else:
                 xo_b = placed("xo_b1", [P, HALF], U8, 2 * BOARD_BYTES)
                 xo_w = placed("xo_w1", [P, HALF], U16, 2 * BOARD_BYTES + HALF)
                 xt_b = placed("xt_b1", [P, HALF], U8, 2 * BOARD_BYTES + 3 * HALF)
-                xt_w = sb_tile("xt_w1", [P, HALF], U32)
+                xt_w = placed("xt_w1", [P, HALF], U32, 2 * BOARD_BYTES + 4 * HALF)
             notes = entries(notes_list, h * HALF, HALF)
             tokens = entries(tokens_list, h * HALF, HALF)
             nc.vector.tensor_copy(xo_b[:], xo_plane[:].indirect(notes))
             nc.vector.tensor_copy(xo_w[:], xo_table[:].indirect(notes))
             nc.vector.tensor_copy(xt_b[:], xt_plane[:].indirect(tokens))
-            nc.vector.tensor_copy(xt_w[:], xt_table[:].indirect(tokens))
+            step = QUARTER if h == 0 else HALF
+            for first in range(0, HALF, step):
+                nc.vector.tensor_copy(
+                    xt_w[:, first : first + step],
+                    xt_table[:].indirect(entries(tokens_list, h * HALF + first, step)),
+                )
             picked.append((xo_w, xo_b, xt_w, xt_b))
 
         a = [sb_tile("a%d" % t, [P, J], F32) for t in range(PACK)]
 
-        def hidden(t, h, copy_out):
-            xo_w, xo_b, xt_w, xt_b = picked[h]
-            acc = psum.tile([P, HALF], F32, name="acc", tag="acc", bufs=4)
+        def bank(width):
+            return psum.tile([P, width], F32, name="bank", tag="bank", bufs=8)
+
+        def hidden(t, first, count, copy_out):
+            xo_w, xo_b, xt_w, xt_b = picked[first // HALF]
+            cols = slice(first % HALF, first % HALF + count)
+            acc = bank(count)
             nc.tensor.matmul_mx(
                 acc[:], lhsT=w2_dealt[:, t, :].bitcast(FP8X4), lhsT_scale=ww_bytes[t][:, 0, :],
-                rhs=xo_w[:].bitcast(FP4X4), rhs_scale=xo_b[:], start=True, stop=False,
+                rhs=xo_w[:, cols].bitcast(FP4X4), rhs_scale=xo_b[:, cols], start=True, stop=False,
             )
             nc.tensor.matmul_mx(
                 acc[:], lhsT=w_dealt[:, t, :].bitcast(FP4X4), lhsT_scale=ww_bytes[t][:, 1, :],
-                rhs=xt_w[:].bitcast(FP8X4), rhs_scale=xt_b[:], start=False, stop=True,
+                rhs=xt_w[:, cols].bitcast(FP8X4), rhs_scale=xt_b[:, cols], start=False, stop=True,
             )
-            copy_out(a[t][:, h * HALF : (h + 1) * HALF], acc[:])
+            copy_out(a[t][:, first : first + count], acc[:])
 
         def put_board(t, first, count):
             nc.scalar.activation(
@@ -195,49 +205,54 @@ def tile_picked_tokens_plain_bank_belowbest_one_plain_kernel(
                 scale=sb_cols[:, t : t + 1],
             )
 
-        woven = {}
+        woven = [sb_tile("woven0", [P, HALF, PACK], BF16, tag="woven")]
+        codes = [sb_tile("codes%d" % h, [P, HALF], U32) for h in range(2)]
+        planes = [sb_tile("plane%d" % h, [P, HALF], U8) for h in range(2)]
+        staged = [[sb_tile("staged%d_%d" % (h, b), [P, HALF], F32) for b in range(N // P)] for h in range(2)]
 
-        def weave(h, pair):
-            if pair == 0:
-                woven[h] = sb_tile("woven%d" % h, [P, HALF, PACK], BF16)
+        def weave(h, pair, cols):
             nc.vector.tensor_copy(
-                woven[h][:, :, 2 * pair : 2 * pair + 2], hid[h, pair][:].rearrange("p t c -> p c t")
+                woven[h][:, cols, 2 * pair : 2 * pair + 2], hid[h, pair][:, :, cols].rearrange("p t c -> p c t")
             )
 
-        def finish(h):
-            codes = sb_tile("codes%d" % h, [P, HALF], U32)
-            plane = sb_tile("plane%d" % h, [P, HALF], U8)
-            nc.vector.quantize_mx(codes[:].bitcast(FP8X4), plane[:], woven[h][:].rearrange("p c t -> p (c t)"))
+        def quantize(h, cols):
+            nc.vector.quantize_mx(
+                codes[h][:, cols].bitcast(FP8X4), planes[h][:, cols],
+                woven[h][:, cols, :].rearrange("p c t -> p (c t)"),
+            )
+
+        def output(h, cols, copies_out):
             for b in range(N // P):
                 rows = slice(b * P, (b + 1) * P)
-                res = psum.tile([P, HALF], F32, name="res", tag="res", bufs=4)
+                res = bank(cols.stop - cols.start)
                 nc.tensor.matmul_mx(
                     res[:], lhsT=wb_codes[:, rows].bitcast(FP8X4), lhsT_scale=wb_plane[:, rows],
-                    rhs=codes[:].bitcast(FP8X4), rhs_scale=plane[:], start=True, stop=True,
+                    rhs=codes[h][:, cols].bitcast(FP8X4), rhs_scale=planes[h][:, cols], start=True, stop=True,
                 )
-                staged = sb_tile("staged%d_%d" % (h, b), [P, HALF], F32)
-                if h == 1 and b == 1:
-                    nc.vector.tensor_copy(staged[:], res[:])
-                else:
-                    nc.scalar.copy(staged[:], res[:])
-                nc.sync.dma_start(out[rows, h * HALF : (h + 1) * HALF], staged[:])
+                copies_out[b](staged[h][b][:, cols], res[:])
+
+        def store(h, b, queue):
+            queue.dma_start(out[b * P : (b + 1) * P, h * HALF : (h + 1) * HALF], staged[h][b][:])
 
         gather_half(0)
-        hidden(0, 0, nc.scalar.copy)
+        hidden(0, 0, QUARTER, nc.scalar.copy)
+        hidden(0, QUARTER, QUARTER, nc.vector.tensor_copy)
         for t in range(1, PACK):
-            hidden(t, 0, nc.vector.tensor_copy)
+            hidden(t, 0, HALF, nc.vector.tensor_copy)
         for b in range(2):
             pw.append(placed("pw%d" % (2 + b), [P, C], F32, b * BOARD_BYTES))
             nc.gpsimd.memset(pw[2 + b][:], 0.0)
-        for t in range(PACK):
+        put_board(0, 0, QUARTER)
+        put_board(0, QUARTER, QUARTER)
+        for t in range(1, PACK):
             put_board(t, 0, HALF)
         gather_half(1)
-        hidden(0, 1, nc.vector.tensor_copy)
+        hidden(0, HALF, HALF, nc.vector.tensor_copy)
         pv.append(sb_tile("pv0", [P, C], F32, tag="xo_table"))
         nc.gpsimd.memset(pv[0][:], 0.0)
-        hidden(1, 1, nc.vector.tensor_copy)
+        hidden(1, HALF, HALF, nc.vector.tensor_copy)
         for t in (2, 3):
-            hidden(t, 1, nc.vector.tensor_copy)
+            hidden(t, HALF, HALF, nc.vector.tensor_copy)
         pv.append(placed("pv1", [P, C], F32, 2 * BOARD_BYTES))
         nc.gpsimd.memset(pv[1][:], 0.0)
 
@@ -255,7 +270,8 @@ def tile_picked_tokens_plain_bank_belowbest_one_plain_kernel(
             merge(t)
             if t in (1, 2):
                 read_places(t - 1, 0)
-        weave(0, 0)
+        whole = slice(0, HALF)
+        weave(0, 0, whole)
 
         hid[1, 0] = placed("hid10", [P, 2, HALF], BF16, MARKS_AT)
         hid[0, 1] = placed("hid01", [P, 2, HALF], BF16, MARKS_AT + 4 * HALF)
@@ -266,7 +282,18 @@ def tile_picked_tokens_plain_bank_belowbest_one_plain_kernel(
         read_places(3, 0)
         read_places(2, 1)
         read_places(3, 1)
-        weave(1, 0)
-        for h in range(2):
-            weave(h, 1)
-            finish(h)
+        weave(0, 1, whole)
+        quantize(0, whole)
+        woven.append(sb_tile("woven1", [P, HALF, PACK], BF16, tag="woven"))
+        weave(1, 0, whole)
+        output(0, whole, (nc.scalar.copy, nc.scalar.copy))
+        for b in range(N // P):
+            store(0, b, nc.sync)
+        pieces = (slice(0, QUARTER), slice(QUARTER, HALF))
+        for cols in pieces:
+            weave(1, 1, cols)
+        for cols in pieces:
+            quantize(1, cols)
+            output(1, cols, (nc.scalar.copy, nc.vector.tensor_copy))
+        store(1, 0, nc.scalar)
+        store(1, 1, nc.sync)

from contextlib import ExitStack

import concourse.mybir as mybir

F32 = mybir.dt.float32
BF16 = mybir.dt.bfloat16
I32 = mybir.dt.int32
U32 = mybir.dt.uint32
U16 = mybir.dt.uint16
U8 = mybir.dt.uint8
FP8X4 = mybir.dt.float8_e4m3fn_x4
FP4X4 = mybir.dt.float4_e2m1fn_x4
COPY = mybir.ActivationFunctionType.Copy
ALU = mybir.AluOpType
AXIS_X = mybir.AxisListType.X

P = 128
PACK = 4
QUADS = 4
K, J, R, T, M, C, O, S, N = 512, 512, 512, 2048, 1024, 1024, 512, 256, 256
HALF = 256
GROUP = 16
QUARTER = 128
BOARD_BYTES = 4 * C
MARKS_AT = 3 * BOARD_BYTES

FLOPS = 2 * K * R * J * 2 + 2 * R * N * O


def tile_picked_tokens_plain_bank_belowbest_one_plain_kernel(
    tc, xt_words, xt_scales, w_words, w_scales, xo_words, xo_scales, w2_words, w2_scales,
    sa, sb, wb_words, wb_scales, offs, offs2, offs3, offs4, offs5, offs6, out,
):
    nc = tc.nc
    with ExitStack() as ctx:
        keep = ctx.enter_context(tc.tile_pool(name="keep", bufs=1))
        shared = ctx.enter_context(tc.tile_pool(name="shared", bufs=1))
        psum = ctx.enter_context(tc.psum_pool(name="psum", bufs=1))

        def sb_tile(name, shape, dtype, tag=None):
            return keep.tile(shape, dtype, name=name, tag=tag or name, align_bytes=64)

        def placed(name, shape, dtype, offset):
            return shared.tile(shape, dtype, name=name, align_bytes=64, offset=offset)

        def load_list(name, src):
            lst = keep.tile([P, src.shape[1]], U16, name=name)
            nc.sync.dma_start(lst[:], src)
            return lst

        def entries(lst, first, count):
            return lst[:, first // GROUP : (first + count) // GROUP]

        def rows_by_quadrant(scales):
            return scales[0].rearrange("(q i) c -> i q c", i=PACK).bitcast(I32)

        def load_plane(plane, scales):
            for q in range(QUADS):
                nc.sync.dma_start(
                    plane[32 * q : 32 * q + PACK, :].bitcast(I32),
                    scales[0, PACK * q : PACK * (q + 1), :].bitcast(I32),
                )

        def spread(plane, stage, q):
            rows = plane[32 * q : 32 * q + PACK, :].bitcast(I32)
            nc.vector.tensor_copy(rows.rearrange("p (a c) -> p a c", a=stage.shape[1]), stage[:, :, q, :])

        xt_plane = sb_tile("xt_plane", [P, T], U8)
        xo_plane = sb_tile("xo_plane", [P, M], U8)
        ww_plane = sb_tile("ww_plane", [P, 2 * R], U8)
        wb_plane = sb_tile("wb_plane", [P, N], U8)
        nc.vector.memset(xt_plane[:, : T // 2].bitcast(I32), 0)
        nc.gpsimd.memset(xt_plane[:, T // 2 :].bitcast(I32), 0)
        for plane in (xo_plane, ww_plane):
            nc.vector.memset(plane[:].bitcast(I32), 0)

        xo_stage = sb_tile("xo_stage", [PACK, 1, QUADS, M // 4], I32)
        ww_stage = sb_tile("ww_stage", [PACK, 2, QUADS, R // 4], I32)
        nc.sync.dma_start(xo_stage[:, 0], rows_by_quadrant(xo_scales))
        nc.sync.dma_start(ww_stage[:, 0], rows_by_quadrant(w2_scales))
        nc.sync.dma_start(ww_stage[:, 1], rows_by_quadrant(w_scales))
        notes_list = load_list("notes_list", offs2)
        tokens_list = load_list("tokens_list", offs)

        xo_table = sb_tile("xo_table", [P, M], U16)
        w2_raw = sb_tile("w2_raw", [P, R], U32)
        w_raw = sb_tile("w_raw", [P, R], U16)
        xt_table = sb_tile("xt_table", [P, T], U32)
        nc.sync.dma_start(xo_table[:].bitcast(I32), xo_words[0].bitcast(I32))
        nc.sync.dma_start(w2_raw[:].bitcast(I32), w2_words[0].rearrange("p c b -> p (c b)").bitcast(I32))
        nc.sync.dma_start(w_raw[:].bitcast(I32), w_words[0].bitcast(I32))
        load_plane(xt_plane, xt_scales)
        nc.sync.dma_start(xt_table[:].bitcast(I32), xt_words[0].rearrange("p c b -> p (c b)").bitcast(I32))

        board_list = load_list("board_list", offs3)
        slot_list = load_list("slot_list", offs4)
        sa_cols = sb_tile("sa_cols", [P, PACK], F32)
        nc.sync.dma_start(sa_cols[:], sa.rearrange("(p t) o -> p (t o)", t=PACK))
        marks_list = load_list("marks_list", offs5)
        places_list = load_list("places_list", offs6)
        sb_cols = sb_tile("sb_cols", [P, PACK], F32)
        nc.sync.dma_start(sb_cols[:], sb.rearrange("(p t) o -> p (t o)", t=PACK))

        for q in range(QUADS):
            spread(xo_plane, xo_stage, q)
            spread(ww_plane, ww_stage, q)

        w2_dealt = sb_tile("w2_dealt", [P, PACK, P], U32)
        w_dealt = sb_tile("w_dealt", [P, PACK, P], U16)
        nc.scalar.copy(w2_dealt[:], w2_raw[:].rearrange("p (m t) -> p t m", t=PACK))
        nc.scalar.copy(w_dealt[:], w_raw[:].rearrange("p (m t) -> p t m", t=PACK))
        ww_bytes = []
        for t in range(PACK):
            dealt = sb_tile("ww_bytes%d" % t, [P, 2, P], U8)
            nc.gpsimd.tensor_copy(dealt[:], ww_plane[:].rearrange("p (a m t) -> p t a m", a=2, t=PACK)[:, t])
            ww_bytes.append(dealt)

        pw = [sb_tile("pw%d" % b, [P, C], F32) for b in range(2)]
        nc.vector.memset(pw[0][:], 0.0)
        nc.gpsimd.memset(pw[1][:], 0.0)

        pv = []
        picked = []

        def gather_half(h):
            if h == 0:
                xo_b = placed("xo_b0", [P, HALF], U8, 0)
                xo_w = placed("xo_w0", [P, HALF], U16, BOARD_BYTES)
                xt_b = placed("xt_b0", [P, HALF], U8, 2 * BOARD_BYTES + 4 * HALF)
                xt_w = placed("xt_w0", [P, HALF], U32, 2 * BOARD_BYTES)
            else:
                xo_b = placed("xo_b1", [P, HALF], U8, 2 * BOARD_BYTES)
                xo_w = placed("xo_w1", [P, HALF], U16, 2 * BOARD_BYTES + HALF)
                xt_b = placed("xt_b1", [P, HALF], U8, 2 * BOARD_BYTES + 3 * HALF)
                xt_w = placed("xt_w1", [P, HALF], U32, 2 * BOARD_BYTES + 4 * HALF)
            notes = entries(notes_list, h * HALF, HALF)
            tokens = entries(tokens_list, h * HALF, HALF)
            nc.vector.tensor_copy(xo_b[:], xo_plane[:].indirect(notes))
            nc.vector.tensor_copy(xo_w[:], xo_table[:].indirect(notes))
            nc.vector.tensor_copy(xt_b[:], xt_plane[:].indirect(tokens))
            step = QUARTER if h == 0 else HALF
            for first in range(0, HALF, step):
                nc.vector.tensor_copy(
                    xt_w[:, first : first + step],
                    xt_table[:].indirect(entries(tokens_list, h * HALF + first, step)),
                )
            picked.append((xo_w, xo_b, xt_w, xt_b))

        a = [sb_tile("a%d" % t, [P, J], F32) for t in range(PACK)]

        def bank(width):
            return psum.tile([P, width], F32, name="bank", tag="bank", bufs=8)

        def hidden(t, first, count, copy_out):
            xo_w, xo_b, xt_w, xt_b = picked[first // HALF]
            cols = slice(first % HALF, first % HALF + count)
            acc = bank(count)
            nc.tensor.matmul_mx(
                acc[:], lhsT=w2_dealt[:, t, :].bitcast(FP8X4), lhsT_scale=ww_bytes[t][:, 0, :],
                rhs=xo_w[:, cols].bitcast(FP4X4), rhs_scale=xo_b[:, cols], start=True, stop=False,
            )
            nc.tensor.matmul_mx(
                acc[:], lhsT=w_dealt[:, t, :].bitcast(FP4X4), lhsT_scale=ww_bytes[t][:, 1, :],
                rhs=xt_w[:, cols].bitcast(FP8X4), rhs_scale=xt_b[:, cols], start=False, stop=True,
            )
            copy_out(a[t][:, first : first + count], acc[:])

        def put_board(t, first, count):
            nc.scalar.activation(
                pw[t][:].indirect(entries(board_list, first, count)), a[t][:, first : first + count], COPY
            )

        h1 = {}

        def take_marks(t):
            if t == PACK - 1:
                h1[t] = placed("h1_last", [P, S], F32, MARKS_AT + 2 * HALF)
            else:
                h1[t] = sb_tile("h1_%d" % t, [P, S], F32)
            nc.scalar.activation(h1[t][:], a[t][:].indirect(slot_list[:]), COPY, scale=sa_cols[:, t : t + 1])

        def put_marks(t):
            nc.scalar.activation(pv[t % 2][:].indirect(marks_list[:]), h1[t][:], COPY)

        pb = {}
        pg = {}

        def row_top(t):
            top = sb_tile("top%d" % t, [P, 1], F32)
            pb[t] = sb_tile("pb%d" % t, [P, 1], F32)
            nc.vector.tensor_reduce(top[:], h1[t][:], AXIS_X, ALU.max)
            nc.vector.tensor_scalar_max(pb[t][:], top[:], 0.0)

        def merge(t):
            pg[t] = sb_tile("pg%d" % t, [P, C], F32)
            nc.vector.scalar_tensor_tensor(
                pg[t][:], pv[t % 2][:], pb[t][:], pw[t][:], ALU.subtract, ALU.max
            )

        hid = {}

        def read_places(t, h):
            nc.scalar.activation(
                hid[h, t // 2][:, t % 2, :], pg[t][:].indirect(entries(places_list, h * HALF, HALF)), COPY,
                scale=sb_cols[:, t : t + 1],
            )

        woven = [sb_tile("woven0", [P, HALF, PACK], BF16, tag="woven")]
        codes = [sb_tile("codes%d" % h, [P, HALF], U32) for h in range(2)]
        planes = [sb_tile("plane%d" % h, [P, HALF], U8) for h in range(2)]
        staged = [[sb_tile("staged%d_%d" % (h, b), [P, HALF], F32) for b in range(N // P)] for h in range(2)]

        def weave(h, pair, cols):
            nc.vector.tensor_copy(
                woven[h][:, cols, 2 * pair : 2 * pair + 2], hid[h, pair][:, :, cols].rearrange("p t c -> p c t")
            )

        def quantize(h, cols):
            nc.vector.quantize_mx(
                codes[h][:, cols].bitcast(FP8X4), planes[h][:, cols],
                woven[h][:, cols, :].rearrange("p c t -> p (c t)"),
            )

        def output(h, cols, copies_out):
            for b in range(N // P):
                rows = slice(b * P, (b + 1) * P)
                res = bank(cols.stop - cols.start)
                nc.tensor.matmul_mx(
                    res[:], lhsT=wb_codes[:, rows].bitcast(FP8X4), lhsT_scale=wb_plane[:, rows],
                    rhs=codes[h][:, cols].bitcast(FP8X4), rhs_scale=planes[h][:, cols], start=True, stop=True,
                )
                copies_out[b](staged[h][b][:, cols], res[:])

        def store(h, b, queue):
            queue.dma_start(out[b * P : (b + 1) * P, h * HALF : (h + 1) * HALF], staged[h][b][:])

        gather_half(0)
        hidden(0, 0, QUARTER, nc.scalar.copy)
        hidden(0, QUARTER, QUARTER, nc.vector.tensor_copy)
        for t in range(1, PACK):
            hidden(t, 0, HALF, nc.vector.tensor_copy)
        for b in range(2):
            pw.append(placed("pw%d" % (2 + b), [P, C], F32, b * BOARD_BYTES))
            nc.gpsimd.memset(pw[2 + b][:], 0.0)
        put_board(0, 0, QUARTER)
        put_board(0, QUARTER, QUARTER)
        for t in range(1, PACK):
            put_board(t, 0, HALF)
        gather_half(1)
        hidden(0, HALF, HALF, nc.vector.tensor_copy)
        pv.append(sb_tile("pv0", [P, C], F32, tag="xo_table"))
        nc.gpsimd.memset(pv[0][:], 0.0)
        hidden(1, HALF, HALF, nc.vector.tensor_copy)
        for t in (2, 3):
            hidden(t, HALF, HALF, nc.vector.tensor_copy)
        pv.append(placed("pv1", [P, C], F32, 2 * BOARD_BYTES))
        nc.gpsimd.memset(pv[1][:], 0.0)

        wb_codes = sb_tile("wb_codes", [P, N], U32)
        nc.sync.dma_start(wb_codes[:].bitcast(I32), wb_words[0].rearrange("p c b -> p (c b)").bitcast(I32))
        nc.vector.memset(wb_plane[:].bitcast(I32), 0)
        load_plane(wb_plane, wb_scales)

        hid[0, 0] = sb_tile("hid00", [P, 2, HALF], BF16)
        for t in range(PACK):
            take_marks(t)
            row_top(t)
            put_board(t, HALF, HALF)
            put_marks(t)
            merge(t)
            if t in (1, 2):
                read_places(t - 1, 0)
        whole = slice(0, HALF)
        weave(0, 0, whole)

        hid[1, 0] = placed("hid10", [P, 2, HALF], BF16, MARKS_AT)
        hid[0, 1] = placed("hid01", [P, 2, HALF], BF16, MARKS_AT + 4 * HALF)
        hid[1, 1] = sb_tile("hid11", [P, 2, HALF], BF16, tag="pb3")
        read_places(0, 1)
        read_places(1, 1)
        read_places(2, 0)
        read_places(3, 0)
        read_places(2, 1)
        read_places(3, 1)
        weave(0, 1, whole)
        quantize(0, whole)
        woven.append(sb_tile("woven1", [P, HALF, PACK], BF16, tag="woven"))
        weave(1, 0, whole)
        output(0, whole, (nc.scalar.copy, nc.scalar.copy))
        for b in range(N // P):
            store(0, b, nc.sync)
        pieces = (slice(0, QUARTER), slice(QUARTER, HALF))
        for cols in pieces:
            weave(1, 1, cols)
        for cols in pieces:
            quantize(1, cols)
            output(1, cols, (nc.scalar.copy, nc.vector.tensor_copy))
        store(1, 0, nc.scalar)
        store(1, 1, nc.sync)
